import numpy as np, ml_dtypes
CORES = [45,53,77,117,47,55,79,119]
N = 8
import mx_ref
NC = 512
EPS = 0.001
BF = ml_dtypes.bfloat16
def setup_inputs(rng):
    def f(*shape):
        return mx_ref.flush((rng.standard_normal(shape, dtype=np.float32) * np.exp2(rng.integers(-2, 3, shape[:-1] + (1,)))).astype(BF))
    return {"x": f(N, 128, 512), "w": f(N, 128, 4 * NC)}
def setup_inputs_blocks(rng):
    d = setup_inputs(rng)
    for k in ("x", "w"): d[k] = mx_ref.spread(d[k], rng, 4)
    return d
def setup_inputs_wide(rng):
    d = setup_inputs(rng)
    for k in ("x", "w"): d[k] = mx_ref.flush((d[k].astype(np.float32) * np.exp2(rng.integers(-6, 7, (N, 1, 1))).astype(np.float32)).astype(BF))
    return d
def setup_inputs_tokens(rng):
    d = setup_inputs(rng); v = d["x"].astype(np.float32).reshape(N, 128, -1, 4)
    d["x"] = mx_ref.flush((v * np.exp2(rng.integers(-6, 7, (N, 1, v.shape[2], 1))).astype(np.float32)).reshape(d["x"].shape).astype(BF))
    return d
def setup_inputs_faint(rng):
    d = setup_inputs(rng); d["x"] = mx_ref.flush((d["x"].astype(np.float32) * np.float32(2.0 ** -12)).astype(BF))
    return d
def reference(x, w):
    W = [mx_ref.quantize(w[r]) for r in range(N)]
    y = np.zeros((N, 128, N * NC), np.float32)
    for j in range(N):
        X = mx_ref.quantize(x[j])
        Z = [mx_ref.matmul(X, W[r]) for r in range(N)]
        ms = sum((z.astype(np.float64) ** 2).sum(axis=1, keepdims=True) for z in Z) / (N * NC)
        for r in range(N):
            y[r][:, NC * j:NC * j + NC] = (Z[r] / np.sqrt(ms + EPS)).astype(np.float32)
    return {"y": y}

@@ -1,0 +1,277 @@
+import math
+from concourse.bass import DstId, RemoteDMATransfer
+from concourse.mybir import dt, AluOpType, ActivationFunctionType
+
+N = 8
+NC = 512
+TOK = 128
+EPS = 0.001
+WP = 2
+NV = 24
+DOWN = 2.0 ** -40
+
+SCRATCH = {
+    "xb": ("sbuf", [128, 4 * TOK], "bfloat16"),
+    "wb": ("sbuf", [128, 4 * NC], "bfloat16"),
+    "xq": ("sbuf", [128, N * TOK], "float8_e4m3fn_x4"),
+    "xs": ("sbuf", [128, N * TOK], "uint8"),
+    "wq": ("sbuf", [128, NC], "float8_e4m3fn_x4"),
+    "ws": ("sbuf", [128, NC], "uint8"),
+    "z": ("psum", [128, N * NC], "float32"),
+    "junk": ("sbuf", [128, N * NC], "float32"),
+    "yb": ("sbuf", [128, N * NC], "float32"),
+    "part": ("sbuf", [128, N], "float32"),
+    "lp": ("sbuf", [128, N], "float32"),
+    "ls0": ("sbuf", [128, N], "float32"),
+    "ls1": ("sbuf", [128, N], "float32"),
+    "ls2": ("sbuf", [128, N], "float32"),
+    "ls3": ("sbuf", [128, N], "float32"),
+    "sd": ("sbuf", [128, N], "float32"),
+    "tmp": ("sbuf", [128, 12 * N], "float32"),
+}
+SEMAPHORES = (["lx", "qx", "sent", "st"] + ["lw%d" % h for h in range(WP)] + ["qw%d" % h for h in range(WP)]
+              + ["%s%d" % (p, j) for p in ("xa", "mm", "sq", "sc") for j in range(N)]
+              + ["sp%d" % k for k in range(2)] + ["sd%d" % k for k in range(2)]
+              + ["sr%d_%d" % (k, c) for k in range(2) for c in range(4)] + ["v%d" % i for i in range(NV)])
+
+
+def _count(m):
+    return sum((m >> e) & 1 for e in range(m.bit_length()))
+
+
+def _plan(cores, topo):
+    n = len(cores)
+    chips = sorted({topo.chip(c) for c in cores})
+    far, near = {}, {}
+    for ch in chips:
+        here = [r for r in range(n) if topo.chip(cores[r]) == ch]
+        free = [r for r in here if all(topo.may_write(cores[r], c) for c in cores if c != cores[r])]
+        far[ch] = free[-1]
+        near[ch] = [r for r in here if r != far[ch]][0]
+    own, oth = {}, {}
+    for ch in chips:
+        rest = [o for o in chips if o != ch]
+        own[ch] = [o for o in rest if topo.may_write(cores[near[ch]], cores[near[o]])]
+        q = [o for o in rest if o not in own[ch]]
+        k = sorted([ch] + own[ch]).index(ch) % max(len(q), 1)
+        oth[ch] = q[k:] + q[:k]
+    gq, order = {}, {}
+    for ch in chips:
+        a, b = near[ch], far[ch]
+        qs = sorted([o for o in chips if ch in oth[o]], key=lambda o: oth[o].index(ch))
+        ps = [o for o in chips if ch in own[o]]
+        come = [far[o] for o in qs] + [near[o] for o in ps] + [far[o] for o in ps]
+        late = [near[o] for o in qs]
+        gq[b] = [("x", b, [near[o] for o in oth[ch]], [a]), ("x", a, [near[o] for o in oth[ch]], []),
+                 ("fold", 0), ("fold", 1)]
+        gq[a] = ([("x", a, [near[o] for o in own[ch]], [b]), ("x", b, [near[o] for o in own[ch]], [])]
+                 + [("x", j, [], [b]) for j in come] + [("part", 0)] + [("x", j, [], [b]) for j in late] + [("part", 1)])
+        order[a] = order[b] = [b, a] + come + late
+    return {"chips": chips, "far": far, "near": near, "own": own, "oth": oth, "gq": gq, "order": order,
+            "groups": [[far[ch] for ch in chips], [near[ch] for ch in chips]]}
+
+
+def _masks(src, offs, ons, cores, topo):
+    m_off = topo.mask(cores[src], cores[offs[0]]) if offs else 0
+    m_on = topo.mask(cores[src], cores[ons[0]]) if ons else 0
+    return m_off, m_on & ~m_off
+
+
+def rank_program(g, core, T, topo):
+    rank = T.rank_of(core)
+    if rank is None:
+        return
+    cores = list(T.cores)
+    P = _plan(cores, topo)
+    S = T.sem
+    chips, groups = P["chips"], P["groups"]
+    ch = topo.chip(core)
+    ci = chips.index(ch)
+    is_far = P["far"][ch] == rank
+    mate = P["near"][ch] if is_far else P["far"][ch]
+    col = {j: k for k, j in enumerate([j for grp in groups for j in grp])}
+    span = []
+    for grp in groups:
+        span.append((col[grp[0]], col[grp[0]] + len(grp)))
+
+    expect = {}
+    for s in range(N):
+        for act in P["gq"][s]:
+            if act[0] == "x":
+                m_off, m_on = _masks(s, act[2], act[3], cores, topo)
+                for d in act[2]:
+                    expect[(d, act[1])] = 2 * _count(m_off)
+                for d in act[3]:
+                    expect[(d, act[1])] = 2 * _count(m_on)
+
+    def did(r):
+        rid, pid, _ = topo.addr(cores[r])
+        return DstId(rid=rid, pnc=pid)
+
+    def tok(j):
+        return slice(TOK * j, TOK * j + TOK)
+
+    def blk(j):
+        return slice(NC * j, NC * j + NC)
+
+    order = P["order"][rank]
+    sy, ve, te, sc = g.sync, g.vector, g.tensor, g.scalar
+
+    sy.dma_start(T.xb[:, :], T.x[:, :]).then_inc(S.lx, 16)
+    wc = 4 * NC // WP
+    for h in range(WP):
+        sy.dma_start(T.wb[:, wc * h:wc * h + wc], T.w[:, wc * h:wc * h + wc]).then_inc(S["lw%d" % h], 16)
+
+    ve.wait_ge(S.lx, 16)
+    ve.quantize_mx(T.xq[:, tok(rank)], T.xs[:, tok(rank)], T.xb[:, :]).then_inc(S.qx, 1)
+    for h in range(WP):
+        ve.wait_ge(S["lw%d" % h], 16)
+        q = NC // WP
+        ve.quantize_mx(T.wq[:, q * h:q * h + q], T.ws[:, q * h:q * h + q],
+                       T.wb[:, wc * h:wc * h + wc]).then_inc(S["qw%d" % h], 1)
+
+    for h in range(WP):
+        te.wait_ge(S["qw%d" % h], 1)
+    for j in order:
+        if j == rank:
+            te.wait_ge(S.qx, 1)
+        else:
+            te.wait_ge(S["xa%d" % j], expect[(rank, j)])
+        te.matmul_mx(T.z[:, blk(j)], T.xq[:, tok(j)], T.xs[:, tok(j)], T.wq[:, :], T.ws[:, :],
+                     True, True).then_inc(S["mm%d" % j], 1)
+
+    sent = 0
+    for act in P["gq"][rank]:
+        if act[0] == "x":
+            j, offs, ons = act[1], act[2], act[3]
+            if j == rank:
+                g.wait_ge(S.qx, 1)
+            else:
+                g.wait_ge(S["xa%d" % j], expect[(rank, j)])
+            m_off, m_on = _masks(rank, offs, ons, cores, topo)
+            for view in (T.xq[:, tok(j)].bitcast(dt.uint8), T.xs[:, tok(j)]):
+                tr = []
+                for m, ds in ((m_off, offs), (m_on, ons)):
+                    if ds:
+                        tr.append(RemoteDMATransfer(dst_ids=[did(d) for d in ds], dma_engine_mask=m,
+                                                    remote_sem=S["xa%d" % j], srcs=[view], dsts=[view] * len(ds),
+                                                    alu_op=0))
+                        sent += _count(m)
+                g.remote_dma_fused(tr, local_sem=S.sent)
+        elif act[0] == "part":
+            k = act[1]
+            c0, c1 = span[k]
+            for j in groups[k]:
+                g.wait_ge(S["sq%d" % j], 1)
+            rid, pid, _ = topo.addr(cores[mate])
+            m = topo.mask(core, cores[mate])
+            g.remote_dma(T.lp[:, c0:c1], T.part[:, c0:c1], S["sp%d" % k], S.sent, pid, rid, m)
+            sent += _count(m)
+        else:
+            k = act[1]
+            c0, c1 = span[k]
+            for j in groups[k]:
+                g.wait_ge(S["sq%d" % j], 1)
+            g.wait_ge(S["sp%d" % k], _count(topo.mask(cores[mate], core)))
+            offs = [r for r in range(N) if topo.chip(cores[r]) != ch]
+            m_off, m_on = _masks(rank, offs, [mate], cores, topo)
+            land = T["ls%d" % ci][:, c0:c1]
+            tr = []
+            for m, ds in ((m_off, offs), (m_on, [mate])):
+                tr.append(RemoteDMATransfer(dst_ids=[did(d) for d in ds], dma_engine_mask=m,
+                                            remote_sem=S["sr%d_%d" % (k, ci)],
+                                            srcs=[T.part[:, c0:c1], T.lp[:, c0:c1]], dsts=[land] * len(ds), alu_op=1))
+                sent += _count(m)
+            g.remote_dma_fused(tr, local_sem=S.sent)
+    g.wait_ge(S.sent, sent)
+
+    nv = [0]
+    slot = [0]
+
+    def vsem():
+        nv[0] += 1
+        return S["v%d" % (nv[0] - 1)]
+
+    def fold_count(src_chip, dst_rank):
+        s = P["far"][src_chip]
+        offs = [r for r in range(N) if topo.chip(cores[r]) != src_chip]
+        m_off, m_on = _masks(s, offs, [P["near"][src_chip]], cores, topo)
+        return _count(m_on) if topo.chip(cores[dst_rank]) == src_chip else _count(m_off)
+
+    tot_sem, r1_sem, tot_ap, r1_ap = {}, {}, {}, {}
+    ADD, MUL = AluOpType.add, AluOpType.mult
+    vec_tail = {}
+    for k, grp in enumerate(groups):
+        c0, c1 = span[k]
+
+        def tv(i):
+            return T.tmp[:, N * i + c0:N * i + c1]
+
+        for j in grp:
+            ve.wait_ge(S["sq%d" % j], 1)
+        others = P["own"][ch] + P["oth"][ch]
+        if is_far:
+            ve.wait_ge(S["sp%d" % k], _count(topo.mask(cores[mate], core)))
+            s = vsem()
+            ve.tensor_tensor(tv(0), T.part[:, c0:c1], T.lp[:, c0:c1], ADD).then_inc(s, 1)
+            acc = tv(0)
+        else:
+            s = S["sr%d_%d" % (k, ci)]
+            acc = T["ls%d" % ci][:, c0:c1]
+        need = 1 if is_far else fold_count(ch, rank)
+        for i, o in enumerate(others):
+            oi = chips.index(o)
+            ve.wait_ge(s, need)
+            ve.wait_ge(S["sr%d_%d" % (k, oi)], fold_count(o, rank))
+            s, need = vsem(), 1
+            ve.tensor_tensor(tv(1 + i), acc, T["ls%d" % oi][:, c0:c1], ADD).then_inc(s, 1)
+            acc = tv(1 + i)
+        tot_sem[k], tot_ap[k] = s, acc
+        ve.wait_ge(s, 1)
+        s_e = vsem()
+        ve.tensor_scalar(tv(5), acc, EPS, None, ADD).then_inc(s_e, 1)
+        ve.wait_ge(S["sd%d" % k], 1)
+        s1 = vsem()
+        ve.reciprocal(tv(6), T.sd[:, c0:c1]).then_inc(s1, 1)
+        ve.wait_ge(s1, 1)
+        s2 = vsem()
+        ve.tensor_tensor(tv(7), tv(6), tv(6), MUL).then_inc(s2, 1)
+        ve.wait_ge(s2, 1)
+        ve.wait_ge(s_e, 1)
+        s3 = vsem()
+        ve.tensor_tensor(tv(8), tv(5), tv(7), MUL).then_inc(s3, 1)
+        ve.wait_ge(s3, 1)
+        s4 = vsem()
+        ve.tensor_scalar(tv(9), tv(8), -0.5 * DOWN * math.sqrt(DOWN), 1.5 * math.sqrt(DOWN), MUL, ADD).then_inc(s4, 1)
+        ve.wait_ge(s4, 1)
+        s5 = vsem()
+        ve.tensor_tensor(tv(10), tv(6), tv(9), MUL).then_inc(s5, 1)
+        r1_sem[k] = s5
+        ve.wait_ge(s5, 1)
+        for i, j in enumerate(grp):
+            if i % 2 == 0:
+                c = N * 10 + col[j]
+                ve.tensor_scalar(T.yb[:, blk(j)], T.z[:, blk(j)], T.tmp[:, c:c + 1], None,
+                                 MUL).then_inc(S["sc%d" % j], 1)
+
+    for j in order:
+        sc.wait_ge(S["mm%d" % j], 1)
+        sc.activation(T.junk[:, blk(j)], T.z[:, blk(j)], ActivationFunctionType.Square,
+                      scale=1.0 / math.sqrt(N * NC), accum_out=T.part[:, col[j]:col[j] + 1]).then_inc(S["sq%d" % j], 1)
+    for k, grp in enumerate(groups):
+        c0, c1 = span[k]
+        sc.wait_ge(tot_sem[k], 1)
+        sc.activation(T.sd[:, c0:c1], tot_ap[k], ActivationFunctionType.Sqrt, bias=EPS * DOWN,
+                      scale=DOWN).then_inc(S["sd%d" % k], 1)
+        sc.wait_ge(r1_sem[k], 1)
+        for i, j in enumerate(grp):
+            if i % 2 == 1:
+                c = N * 10 + col[j]
+                sc.activation(T.yb[:, blk(j)], T.z[:, blk(j)], ActivationFunctionType.Copy,
+                              scale=T.tmp[:, c:c + 1]).then_inc(S["sc%d" % j], 1)
+
+    for grp in groups:
+        for j in grp:
+            sy.wait_ge(S["sc%d" % j], 1)
+            sy.dma_start(T.y[:, blk(j)], T.yb[:, blk(j)]).then_inc(S.st, 16)
+    sy.wait_ge(S.st, 16 * N)

@@ -21,6 +21,8 @@ SCRATCH = {
     "junk": ("sbuf", [128, N * NC], "float32"),
     "yb": ("sbuf", [128, N * NC], "float32"),
     "part": ("sbuf", [128, N], "float32"),
+    "pe": ("sbuf", [128, N], "float32"),
+    "cs": ("sbuf", [128, N], "float32"),
     "lp": ("sbuf", [128, N], "float32"),
     "ls0": ("sbuf", [128, N], "float32"),
     "ls1": ("sbuf", [128, N], "float32"),
@@ -30,8 +32,8 @@ SCRATCH = {
     "tmp": ("sbuf", [128, 12 * N], "float32"),
 }
 SEMAPHORES = (["lx", "qx", "sent", "st"] + ["lw%d" % h for h in range(WP)] + ["qw%d" % h for h in range(WP)]
-              + ["%s%d" % (p, j) for p in ("xa", "mm", "sq", "sc") for j in range(N)]
-              + ["sp%d" % k for k in range(2)] + ["sd%d" % k for k in range(2)]
+              + ["%s%d" % (p, j) for p in ("xc", "xp", "mm", "sq", "sc") for j in range(N)]
+              + ["%s%d" % (p, k) for p in ("sp", "sd", "loc") for k in range(2)]
               + ["sr%d_%d" % (k, c) for k in range(2) for c in range(4)] + ["v%d" % i for i in range(NV)])
 
 
@@ -60,13 +62,14 @@ def _plan(cores, topo):
         a, b = near[ch], far[ch]
         qs = sorted([o for o in chips if ch in oth[o]], key=lambda o: oth[o].index(ch))
         ps = [o for o in chips if ch in own[o]]
-        come = [far[o] for o in qs] + [near[o] for o in ps] + [far[o] for o in ps]
+        come = [near[o] for o in ps] + [far[o] for o in qs] + [far[o] for o in ps]
         late = [near[o] for o in qs]
-        gq[b] = [("x", b, [near[o] for o in oth[ch]], [a]), ("x", a, [near[o] for o in oth[ch]], []),
-                 ("fold", 0), ("fold", 1)]
-        gq[a] = ([("x", a, [near[o] for o in own[ch]], [b]), ("x", b, [near[o] for o in own[ch]], [])]
+        gq[b] = [("x", b, [near[o] for o in oth[ch] + own[ch]], [a]), ("x", a, [near[o] for o in oth[ch]], []),
+                 ("sum", 0), ("sum", 1)]
+        gq[a] = ([("x", a, [near[o] for o in own[ch]], [b])]
                  + [("x", j, [], [b]) for j in come] + [("part", 0)] + [("x", j, [], [b]) for j in late] + [("part", 1)])
-        order[a] = order[b] = [b, a] + come + late
+        order[a] = [a, b] + come + late
+        order[b] = [b, a] + come + late
     return {"chips": chips, "far": far, "near": near, "own": own, "oth": oth, "gq": gq, "order": order,
             "groups": [[far[ch] for ch in chips], [near[ch] for ch in chips]]}
 
@@ -100,9 +103,9 @@ def rank_program(g, core, T, topo):
             if act[0] == "x":
                 m_off, m_on = _masks(s, act[2], act[3], cores, topo)
                 for d in act[2]:
-                    expect[(d, act[1])] = 2 * _count(m_off)
+                    expect[(d, act[1])] = _count(m_off)
                 for d in act[3]:
-                    expect[(d, act[1])] = 2 * _count(m_on)
+                    expect[(d, act[1])] = _count(m_on)
 
     def did(r):
         rid, pid, _ = topo.addr(cores[r])
@@ -116,6 +119,7 @@ def rank_program(g, core, T, topo):
 
     order = P["order"][rank]
     sy, ve, te, sc = g.sync, g.vector, g.tensor, g.scalar
+    ADD, MUL = AluOpType.add, AluOpType.mult
 
     sy.dma_start(T.xb[:, :], T.x[:, :]).then_inc(S.lx, 16)
     wc = 4 * NC // WP
@@ -136,7 +140,8 @@ def rank_program(g, core, T, topo):
         if j == rank:
             te.wait_ge(S.qx, 1)
         else:
-            te.wait_ge(S["xa%d" % j], expect[(rank, j)])
+            te.wait_ge(S["xc%d" % j], expect[(rank, j)])
+            te.wait_ge(S["xp%d" % j], expect[(rank, j)])
         te.matmul_mx(T.z[:, blk(j)], T.xq[:, tok(j)], T.xs[:, tok(j)], T.wq[:, :], T.ws[:, :],
                      True, True).then_inc(S["mm%d" % j], 1)
 
@@ -146,33 +151,30 @@ def rank_program(g, core, T, topo):
             j, offs, ons = act[1], act[2], act[3]
             if j == rank:
                 g.wait_ge(S.qx, 1)
-            else:
-                g.wait_ge(S["xa%d" % j], expect[(rank, j)])
             m_off, m_on = _masks(rank, offs, ons, cores, topo)
-            for view in (T.xq[:, tok(j)].bitcast(dt.uint8), T.xs[:, tok(j)]):
+            for name, view in (("xc%d" % j, T.xq[:, tok(j)].bitcast(dt.uint8)), ("xp%d" % j, T.xs[:, tok(j)])):
+                if j != rank:
+                    g.wait_ge(S[name], expect[(rank, j)])
                 tr = []
                 for m, ds in ((m_off, offs), (m_on, ons)):
                     if ds:
                         tr.append(RemoteDMATransfer(dst_ids=[did(d) for d in ds], dma_engine_mask=m,
-                                                    remote_sem=S["xa%d" % j], srcs=[view], dsts=[view] * len(ds),
+                                                    remote_sem=S[name], srcs=[view], dsts=[view] * len(ds),
                                                     alu_op=0))
                         sent += _count(m)
                 g.remote_dma_fused(tr, local_sem=S.sent)
         elif act[0] == "part":
             k = act[1]
             c0, c1 = span[k]
-            for j in groups[k]:
-                g.wait_ge(S["sq%d" % j], 1)
+            g.wait_ge(S["loc%d" % k], 1)
             rid, pid, _ = topo.addr(cores[mate])
             m = topo.mask(core, cores[mate])
-            g.remote_dma(T.lp[:, c0:c1], T.part[:, c0:c1], S["sp%d" % k], S.sent, pid, rid, m)
+            g.remote_dma(T.lp[:, c0:c1], T.pe[:, c0:c1], S["sp%d" % k], S.sent, pid, rid, m)
             sent += _count(m)
         else:
             k = act[1]
             c0, c1 = span[k]
-            for j in groups[k]:
-                g.wait_ge(S["sq%d" % j], 1)
-            g.wait_ge(S["sp%d" % k], _count(topo.mask(cores[mate], core)))
+            g.wait_ge(S["loc%d" % k], 1)
             offs = [r for r in range(N) if topo.chip(cores[r]) != ch]
             m_off, m_on = _masks(rank, offs, [mate], cores, topo)
             land = T["ls%d" % ci][:, c0:c1]
@@ -180,73 +182,72 @@ def rank_program(g, core, T, topo):
             for m, ds in ((m_off, offs), (m_on, [mate])):
                 tr.append(RemoteDMATransfer(dst_ids=[did(d) for d in ds], dma_engine_mask=m,
                                             remote_sem=S["sr%d_%d" % (k, ci)],
-                                            srcs=[T.part[:, c0:c1], T.lp[:, c0:c1]], dsts=[land] * len(ds), alu_op=1))
+                                            srcs=[T.cs[:, c0:c1]], dsts=[land] * len(ds), alu_op=0))
                 sent += _count(m)
             g.remote_dma_fused(tr, local_sem=S.sent)
     g.wait_ge(S.sent, sent)
 
     nv = [0]
-    slot = [0]
 
     def vsem():
         nv[0] += 1
         return S["v%d" % (nv[0] - 1)]
 
-    def fold_count(src_chip, dst_rank):
+    def sum_count(src_chip, dst_rank):
         s = P["far"][src_chip]
         offs = [r for r in range(N) if topo.chip(cores[r]) != src_chip]
         m_off, m_on = _masks(s, offs, [P["near"][src_chip]], cores, topo)
         return _count(m_on) if topo.chip(cores[dst_rank]) == src_chip else _count(m_off)
 
-    tot_sem, r1_sem, tot_ap, r1_ap = {}, {}, {}, {}
-    ADD, MUL = AluOpType.add, AluOpType.mult
-    vec_tail = {}
+    for k, grp in enumerate(groups):
+        c0, c1 = span[k]
+        for j in grp:
+            ve.wait_ge(S["sq%d" % j], 1)
+        if is_far:
+            ve.wait_ge(S["sp%d" % k], _count(topo.mask(cores[mate], core)))
+            ve.tensor_tensor(T.cs[:, c0:c1], T.part[:, c0:c1], T.lp[:, c0:c1], ADD).then_inc(S["loc%d" % k], 1)
+        else:
+            ve.tensor_scalar(T.pe[:, c0:c1], T.part[:, c0:c1], EPS * DOWN / len(chips), None,
+                             ADD).then_inc(S["loc%d" % k], 1)
+
+    tot_sem, f_sem, tot_ap = {}, {}, {}
+    R = math.sqrt(DOWN)
     for k, grp in enumerate(groups):
         c0, c1 = span[k]
 
         def tv(i):
             return T.tmp[:, N * i + c0:N * i + c1]
 
-        for j in grp:
-            ve.wait_ge(S["sq%d" % j], 1)
         others = P["own"][ch] + P["oth"][ch]
         if is_far:
-            ve.wait_ge(S["sp%d" % k], _count(topo.mask(cores[mate], core)))
-            s = vsem()
-            ve.tensor_tensor(tv(0), T.part[:, c0:c1], T.lp[:, c0:c1], ADD).then_inc(s, 1)
-            acc = tv(0)
+            s, need, acc = S["loc%d" % k], 1, T.cs[:, c0:c1]
         else:
-            s = S["sr%d_%d" % (k, ci)]
-            acc = T["ls%d" % ci][:, c0:c1]
-        need = 1 if is_far else fold_count(ch, rank)
+            s, need, acc = S["sr%d_%d" % (k, ci)], sum_count(ch, rank), T["ls%d" % ci][:, c0:c1]
         for i, o in enumerate(others):
             oi = chips.index(o)
             ve.wait_ge(s, need)
-            ve.wait_ge(S["sr%d_%d" % (k, oi)], fold_count(o, rank))
+            ve.wait_ge(S["sr%d_%d" % (k, oi)], sum_count(o, rank))
             s, need = vsem(), 1
             ve.tensor_tensor(tv(1 + i), acc, T["ls%d" % oi][:, c0:c1], ADD).then_inc(s, 1)
             acc = tv(1 + i)
         tot_sem[k], tot_ap[k] = s, acc
         ve.wait_ge(s, 1)
-        s_e = vsem()
-        ve.tensor_scalar(tv(5), acc, EPS, None, ADD).then_inc(s_e, 1)
-        ve.wait_ge(S["sd%d" % k], 1)
         s1 = vsem()
-        ve.reciprocal(tv(6), T.sd[:, c0:c1]).then_inc(s1, 1)
+        ve.reciprocal(tv(5), acc).then_inc(s1, 1)
         ve.wait_ge(s1, 1)
+        ve.wait_ge(S["sd%d" % k], 1)
         s2 = vsem()
-        ve.tensor_tensor(tv(7), tv(6), tv(6), MUL).then_inc(s2, 1)
+        ve.tensor_tensor(tv(6), T.sd[:, c0:c1], tv(5), MUL).then_inc(s2, 1)
         ve.wait_ge(s2, 1)
-        ve.wait_ge(s_e, 1)
         s3 = vsem()
-        ve.tensor_tensor(tv(8), tv(5), tv(7), MUL).then_inc(s3, 1)
+        ve.tensor_tensor(tv(7), tv(6), T.sd[:, c0:c1], MUL).then_inc(s3, 1)
         ve.wait_ge(s3, 1)
         s4 = vsem()
-        ve.tensor_scalar(tv(9), tv(8), -0.5 * DOWN * math.sqrt(DOWN), 1.5 * math.sqrt(DOWN), MUL, ADD).then_inc(s4, 1)
+        ve.tensor_scalar(tv(8), tv(7), -0.5 * R, 1.5 * R, MUL, ADD).then_inc(s4, 1)
         ve.wait_ge(s4, 1)
         s5 = vsem()
-        ve.tensor_tensor(tv(10), tv(6), tv(9), MUL).then_inc(s5, 1)
-        r1_sem[k] = s5
+        ve.tensor_tensor(tv(10), tv(6), tv(8), MUL).then_inc(s5, 1)
+        f_sem[k] = s5
         ve.wait_ge(s5, 1)
         for i, j in enumerate(grp):
             if i % 2 == 0:
@@ -257,21 +258,30 @@ def rank_program(g, core, T, topo):
     for j in order:
         sc.wait_ge(S["mm%d" % j], 1)
         sc.activation(T.junk[:, blk(j)], T.z[:, blk(j)], ActivationFunctionType.Square,
-                      scale=1.0 / math.sqrt(N * NC), accum_out=T.part[:, col[j]:col[j] + 1]).then_inc(S["sq%d" % j], 1)
+                      scale=math.sqrt(DOWN / (N * NC)), accum_out=T.part[:, col[j]:col[j] + 1]).then_inc(S["sq%d" % j], 1)
     for k, grp in enumerate(groups):
         c0, c1 = span[k]
         sc.wait_ge(tot_sem[k], 1)
-        sc.activation(T.sd[:, c0:c1], tot_ap[k], ActivationFunctionType.Sqrt, bias=EPS * DOWN,
-                      scale=DOWN).then_inc(S["sd%d" % k], 1)
-        sc.wait_ge(r1_sem[k], 1)
+        sc.activation(T.sd[:, c0:c1], tot_ap[k], ActivationFunctionType.Sqrt).then_inc(S["sd%d" % k], 1)
+        sc.wait_ge(f_sem[k], 1)
         for i, j in enumerate(grp):
             if i % 2 == 1:
                 c = N * 10 + col[j]
                 sc.activation(T.yb[:, blk(j)], T.z[:, blk(j)], ActivationFunctionType.Copy,
                               scale=T.tmp[:, c:c + 1]).then_inc(S["sc%d" % j], 1)
 
+    st = 0
     for grp in groups:
-        for j in grp:
-            sy.wait_ge(S["sc%d" % j], 1)
-            sy.dma_start(T.y[:, blk(j)], T.yb[:, blk(j)]).then_inc(S.st, 16)
-    sy.wait_ge(S.st, 16 * N)
+        for i in range(0, len(grp), 2):
+            pair = grp[i:i + 2]
+            for j in pair:
+                sy.wait_ge(S["sc%d" % j], 1)
+            if len(pair) == 2 and pair[1] == pair[0] + 1:
+                lo, hi = NC * pair[0], NC * pair[1] + NC
+                sy.dma_start(T.y[:, lo:hi], T.yb[:, lo:hi]).then_inc(S.st, 16)
+                st += 16
+            else:
+                for j in pair:
+                    sy.dma_start(T.y[:, blk(j)], T.yb[:, blk(j)]).then_inc(S.st, 16)
+                    st += 16
+    sy.wait_ge(S.st, st)

@@ -7,8 +7,9 @@ NC = 512
 TOK = 128
 EPS = 0.001
 WP = 2
-NV = 24
+NV = 28
 DOWN = 2.0 ** -40
+FLOOR = 2.0 ** -28
 
 SCRATCH = {
     "xb": ("sbuf", [128, 4 * TOK], "bfloat16"),
@@ -22,16 +23,14 @@ SCRATCH = {
     "yb": ("sbuf", [128, N * NC], "float32"),
     "part": ("sbuf", [128, N], "float32"),
     "pe": ("sbuf", [128, N], "float32"),
-    "cs": ("sbuf", [128, N], "float32"),
     "lp": ("sbuf", [128, N], "float32"),
-    "ls0": ("sbuf", [128, N], "float32"),
-    "ls1": ("sbuf", [128, N], "float32"),
-    "ls2": ("sbuf", [128, N], "float32"),
-    "ls3": ("sbuf", [128, N], "float32"),
+    "L": ("sbuf", [128, 4 * N], "float32"),
+    "tw": ("sbuf", [128, 2 * N], "float32"),
     "sd": ("sbuf", [128, N], "float32"),
-    "tmp": ("sbuf", [128, 12 * N], "float32"),
+    "er": ("sbuf", [128, N], "float32"),
+    "tmp": ("sbuf", [128, 16 * N], "float32"),
 }
-SEMAPHORES = (["lx", "qx", "sent", "st"] + ["lw%d" % h for h in range(WP)] + ["qw%d" % h for h in range(WP)]
+SEMAPHORES = (["lx", "qx", "sent", "st", "er"] + ["lw%d" % h for h in range(WP)] + ["qw%d" % h for h in range(WP)]
               + ["%s%d" % (p, j) for p in ("xc", "xp", "mm", "sq", "sc") for j in range(N)]
               + ["%s%d" % (p, k) for p in ("sp", "sd", "loc") for k in range(2)]
               + ["sr%d_%d" % (k, c) for k in range(2) for c in range(4)] + ["v%d" % i for i in range(NV)])
@@ -96,6 +95,11 @@ def rank_program(g, core, T, topo):
     span = []
     for grp in groups:
         span.append((col[grp[0]], col[grp[0]] + len(grp)))
+    G = len(groups[0])
+    W = G * len(chips)
+
+    def slot(k, c):
+        return T.L[:, W * k + G * c:W * k + G * c + G]
 
     expect = {}
     for s in range(N):
@@ -173,16 +177,14 @@ def rank_program(g, core, T, topo):
             sent += _count(m)
         else:
             k = act[1]
-            c0, c1 = span[k]
             g.wait_ge(S["loc%d" % k], 1)
             offs = [r for r in range(N) if topo.chip(cores[r]) != ch]
             m_off, m_on = _masks(rank, offs, [mate], cores, topo)
-            land = T["ls%d" % ci][:, c0:c1]
             tr = []
             for m, ds in ((m_off, offs), (m_on, [mate])):
                 tr.append(RemoteDMATransfer(dst_ids=[did(d) for d in ds], dma_engine_mask=m,
                                             remote_sem=S["sr%d_%d" % (k, ci)],
-                                            srcs=[T.cs[:, c0:c1]], dsts=[land] * len(ds), alu_op=0))
+                                            srcs=[slot(k, ci)], dsts=[slot(k, ci)] * len(ds), alu_op=0))
                 sent += _count(m)
             g.remote_dma_fused(tr, local_sem=S.sent)
     g.wait_ge(S.sent, sent)
@@ -199,39 +201,59 @@ def rank_program(g, core, T, topo):
         m_off, m_on = _masks(s, offs, [P["near"][src_chip]], cores, topo)
         return _count(m_on) if topo.chip(cores[dst_rank]) == src_chip else _count(m_off)
 
+    e0, e1 = span[0]
+    held = slot(0, ci) if is_far else T.pe[:, e0:e1]
+    rho, rho2 = (T.tmp[:, N * i + e0:N * i + e1] for i in (4, 9))
     for k, grp in enumerate(groups):
         c0, c1 = span[k]
         for j in grp:
             ve.wait_ge(S["sq%d" % j], 1)
         if is_far:
             ve.wait_ge(S["sp%d" % k], _count(topo.mask(cores[mate], core)))
-            ve.tensor_tensor(T.cs[:, c0:c1], T.part[:, c0:c1], T.lp[:, c0:c1], ADD).then_inc(S["loc%d" % k], 1)
+            ve.tensor_tensor(slot(k, ci), T.part[:, c0:c1], T.lp[:, c0:c1], ADD).then_inc(S["loc%d" % k], 1)
         else:
             ve.tensor_scalar(T.pe[:, c0:c1], T.part[:, c0:c1], EPS * DOWN / len(chips), None,
                              ADD).then_inc(S["loc%d" % k], 1)
+        if k == 0:
+            ve.wait_ge(S.er, 1)
+            sa = vsem()
+            ve.reciprocal(rho, T.er[:, e0:e1]).then_inc(sa, 1)
+            ve.wait_ge(sa, 1)
+            sb = vsem()
+            ve.tensor_tensor(rho2, rho, rho, MUL).then_inc(sb, 1)
+            ve.wait_ge(sb, 1)
 
-    tot_sem, f_sem, tot_ap = {}, {}, {}
+    tot_sem, tot_need, f_sem, tot_ap = {}, {}, {}, {}
     R = math.sqrt(DOWN)
+    H = W // 2
     for k, grp in enumerate(groups):
         c0, c1 = span[k]
 
         def tv(i):
             return T.tmp[:, N * i + c0:N * i + c1]
 
-        others = P["own"][ch] + P["oth"][ch]
-        if is_far:
-            s, need, acc = S["loc%d" % k], 1, T.cs[:, c0:c1]
-        else:
-            s, need, acc = S["sr%d_%d" % (k, ci)], sum_count(ch, rank), T["ls%d" % ci][:, c0:c1]
-        for i, o in enumerate(others):
-            oi = chips.index(o)
-            ve.wait_ge(s, need)
-            ve.wait_ge(S["sr%d_%d" % (k, oi)], sum_count(o, rank))
-            s, need = vsem(), 1
-            ve.tensor_tensor(tv(1 + i), acc, T["ls%d" % oi][:, c0:c1], ADD).then_inc(s, 1)
-            acc = tv(1 + i)
-        tot_sem[k], tot_ap[k] = s, acc
+        for oi, o in enumerate(chips):
+            if o == ch and is_far:
+                ve.wait_ge(S["loc%d" % k], 1)
+            else:
+                ve.wait_ge(S["sr%d_%d" % (k, oi)], sum_count(o, rank))
+        s = vsem()
+        ve.tensor_tensor(T.tw[:, H * k:H * k + H], T.L[:, W * k:W * k + H], T.L[:, W * k + H:W * k + W],
+                         ADD).then_inc(s, 1)
         ve.wait_ge(s, 1)
+        s = vsem()
+        acc = tv(11)
+        if k == 0:
+            for i in range(G):
+                a = H * k + i
+                ve.tensor_scalar(T.tmp[:, N * 11 + c0 + i:N * 11 + c0 + i + 1], T.tw[:, a:a + 1], T.tw[:, a + G:a + G + 1],
+                                 T.tmp[:, N * 9 + e0 + i:N * 9 + e0 + i + 1], ADD, MUL).then_inc(s, 1)
+            need = G
+        else:
+            ve.tensor_tensor(acc, T.tw[:, H * k:H * k + G], T.tw[:, H * k + G:H * k + H], ADD).then_inc(s, 1)
+            need = 1
+        tot_sem[k], tot_need[k], tot_ap[k] = s, need, acc
+        ve.wait_ge(s, need)
         s1 = vsem()
         ve.reciprocal(tv(5), acc).then_inc(s1, 1)
         ve.wait_ge(s1, 1)
@@ -241,12 +263,19 @@ def rank_program(g, core, T, topo):
         ve.wait_ge(s2, 1)
         s3 = vsem()
         ve.tensor_tensor(tv(7), tv(6), T.sd[:, c0:c1], MUL).then_inc(s3, 1)
+        lead = tv(6)
+        if k == 0:
+            s6 = vsem()
+            ve.tensor_tensor(tv(12), tv(6), rho, MUL).then_inc(s6, 1)
+            lead = tv(12)
         ve.wait_ge(s3, 1)
         s4 = vsem()
         ve.tensor_scalar(tv(8), tv(7), -0.5 * R, 1.5 * R, MUL, ADD).then_inc(s4, 1)
         ve.wait_ge(s4, 1)
+        if k == 0:
+            ve.wait_ge(s6, 1)
         s5 = vsem()
-        ve.tensor_tensor(tv(10), tv(6), tv(8), MUL).then_inc(s5, 1)
+        ve.tensor_tensor(tv(10), lead, tv(8), MUL).then_inc(s5, 1)
         f_sem[k] = s5
         ve.wait_ge(s5, 1)
         for i, j in enumerate(grp):
@@ -255,13 +284,17 @@ def rank_program(g, core, T, topo):
                 ve.tensor_scalar(T.yb[:, blk(j)], T.z[:, blk(j)], T.tmp[:, c:c + 1], None,
                                  MUL).then_inc(S["sc%d" % j], 1)
 
-    for j in order:
+    last0 = max(order.index(j) for j in groups[0])
+    for n_, j in enumerate(order):
         sc.wait_ge(S["mm%d" % j], 1)
         sc.activation(T.junk[:, blk(j)], T.z[:, blk(j)], ActivationFunctionType.Square,
                       scale=math.sqrt(DOWN / (N * NC)), accum_out=T.part[:, col[j]:col[j] + 1]).then_inc(S["sq%d" % j], 1)
+        if n_ == last0:
+            sc.wait_ge(S.loc0, 1)
+            sc.activation(T.er[:, e0:e1], held, ActivationFunctionType.Sqrt, bias=FLOOR).then_inc(S.er, 1)
     for k, grp in enumerate(groups):
         c0, c1 = span[k]
-        sc.wait_ge(tot_sem[k], 1)
+        sc.wait_ge(tot_sem[k], tot_need[k])
         sc.activation(T.sd[:, c0:c1], tot_ap[k], ActivationFunctionType.Sqrt).then_inc(S["sd%d" % k], 1)
         sc.wait_ge(f_sem[k], 1)
         for i, j in enumerate(grp):

import math
from concourse.bass import DstId, RemoteDMATransfer
from concourse.mybir import dt, AluOpType, ActivationFunctionType

N = 8
NC = 512
TOK = 128
EPS = 0.001
WP = 2
NV = 28
DOWN = 2.0 ** -40
FLOOR = 2.0 ** -28

SCRATCH = {
    "xb": ("sbuf", [128, 4 * TOK], "bfloat16"),
    "wb": ("sbuf", [128, 4 * NC], "bfloat16"),
    "xq": ("sbuf", [128, N * TOK], "float8_e4m3fn_x4"),
    "xs": ("sbuf", [128, N * TOK], "uint8"),
    "wq": ("sbuf", [128, NC], "float8_e4m3fn_x4"),
    "ws": ("sbuf", [128, NC], "uint8"),
    "z": ("psum", [128, N * NC], "float32"),
    "junk": ("sbuf", [128, N * NC], "float32"),
    "yb": ("sbuf", [128, N * NC], "float32"),
    "part": ("sbuf", [128, N], "float32"),
    "pe": ("sbuf", [128, N], "float32"),
    "lp": ("sbuf", [128, N], "float32"),
    "L": ("sbuf", [128, 4 * N], "float32"),
    "tw": ("sbuf", [128, 2 * N], "float32"),
    "sd": ("sbuf", [128, N], "float32"),
    "er": ("sbuf", [128, N], "float32"),
    "tmp": ("sbuf", [128, 16 * N], "float32"),
}
SEMAPHORES = (["lx", "qx", "sent", "st", "er"] + ["lw%d" % h for h in range(WP)] + ["qw%d" % h for h in range(WP)]
              + ["%s%d" % (p, j) for p in ("xc", "xp", "mm", "sq", "sc") for j in range(N)]
              + ["%s%d" % (p, k) for p in ("sp", "sd", "loc") for k in range(2)]
              + ["sr%d_%d" % (k, c) for k in range(2) for c in range(4)] + ["v%d" % i for i in range(NV)])


def _count(m):
    return sum((m >> e) & 1 for e in range(m.bit_length()))


def _plan(cores, topo):
    n = len(cores)
    chips = sorted({topo.chip(c) for c in cores})
    far, near = {}, {}
    for ch in chips:
        here = [r for r in range(n) if topo.chip(cores[r]) == ch]
        free = [r for r in here if all(topo.may_write(cores[r], c) for c in cores if c != cores[r])]
        far[ch] = free[-1]
        near[ch] = [r for r in here if r != far[ch]][0]
    own, oth = {}, {}
    for ch in chips:
        rest = [o for o in chips if o != ch]
        own[ch] = [o for o in rest if topo.may_write(cores[near[ch]], cores[near[o]])]
        q = [o for o in rest if o not in own[ch]]
        k = sorted([ch] + own[ch]).index(ch) % max(len(q), 1)
        oth[ch] = q[k:] + q[:k]
    gq, order = {}, {}
    for ch in chips:
        a, b = near[ch], far[ch]
        qs = sorted([o for o in chips if ch in oth[o]], key=lambda o: oth[o].index(ch))
        ps = [o for o in chips if ch in own[o]]
        come = [near[o] for o in ps] + [far[o] for o in qs] + [far[o] for o in ps]
        late = [near[o] for o in qs]
        gq[b] = [("x", b, [near[o] for o in oth[ch] + own[ch]], [a]), ("x", a, [near[o] for o in oth[ch]], []),
                 ("sum", 0), ("sum", 1)]
        gq[a] = ([("x", a, [near[o] for o in own[ch]], [b])]
                 + [("x", j, [], [b]) for j in come] + [("part", 0)] + [("x", j, [], [b]) for j in late] + [("part", 1)])
        order[a] = [a, b] + come + late
        order[b] = [b, a] + come + late
    return {"chips": chips, "far": far, "near": near, "own": own, "oth": oth, "gq": gq, "order": order,
            "groups": [[far[ch] for ch in chips], [near[ch] for ch in chips]]}


def _masks(src, offs, ons, cores, topo):
    m_off = topo.mask(cores[src], cores[offs[0]]) if offs else 0
    m_on = topo.mask(cores[src], cores[ons[0]]) if ons else 0
    return m_off, m_on & ~m_off


def rank_program(g, core, T, topo):
    rank = T.rank_of(core)
    if rank is None:
        return
    cores = list(T.cores)
    P = _plan(cores, topo)
    S = T.sem
    chips, groups = P["chips"], P["groups"]
    ch = topo.chip(core)
    ci = chips.index(ch)
    is_far = P["far"][ch] == rank
    mate = P["near"][ch] if is_far else P["far"][ch]
    col = {j: k for k, j in enumerate([j for grp in groups for j in grp])}
    span = []
    for grp in groups:
        span.append((col[grp[0]], col[grp[0]] + len(grp)))
    G = len(groups[0])
    W = G * len(chips)

    def slot(k, c):
        return T.L[:, W * k + G * c:W * k + G * c + G]

    expect = {}
    for s in range(N):
        for act in P["gq"][s]:
            if act[0] == "x":
                m_off, m_on = _masks(s, act[2], act[3], cores, topo)
                for d in act[2]:
                    expect[(d, act[1])] = _count(m_off)
                for d in act[3]:
                    expect[(d, act[1])] = _count(m_on)

    def did(r):
        rid, pid, _ = topo.addr(cores[r])
        return DstId(rid=rid, pnc=pid)

    def tok(j):
        return slice(TOK * j, TOK * j + TOK)

    def blk(j):
        return slice(NC * j, NC * j + NC)

    order = P["order"][rank]
    sy, ve, te, sc = g.sync, g.vector, g.tensor, g.scalar
    ADD, MUL = AluOpType.add, AluOpType.mult

    sy.dma_start(T.xb[:, :], T.x[:, :]).then_inc(S.lx, 16)
    wc = 4 * NC // WP
    for h in range(WP):
        sy.dma_start(T.wb[:, wc * h:wc * h + wc], T.w[:, wc * h:wc * h + wc]).then_inc(S["lw%d" % h], 16)

    ve.wait_ge(S.lx, 16)
    ve.quantize_mx(T.xq[:, tok(rank)], T.xs[:, tok(rank)], T.xb[:, :]).then_inc(S.qx, 1)
    for h in range(WP):
        ve.wait_ge(S["lw%d" % h], 16)
        q = NC // WP
        ve.quantize_mx(T.wq[:, q * h:q * h + q], T.ws[:, q * h:q * h + q],
                       T.wb[:, wc * h:wc * h + wc]).then_inc(S["qw%d" % h], 1)

    for h in range(WP):
        te.wait_ge(S["qw%d" % h], 1)
    for j in order:
        if j == rank:
            te.wait_ge(S.qx, 1)
        else:
            te.wait_ge(S["xc%d" % j], expect[(rank, j)])
            te.wait_ge(S["xp%d" % j], expect[(rank, j)])
        te.matmul_mx(T.z[:, blk(j)], T.xq[:, tok(j)], T.xs[:, tok(j)], T.wq[:, :], T.ws[:, :],
                     True, True).then_inc(S["mm%d" % j], 1)

    sent = 0
    for act in P["gq"][rank]:
        if act[0] == "x":
            j, offs, ons = act[1], act[2], act[3]
            if j == rank:
                g.wait_ge(S.qx, 1)
            m_off, m_on = _masks(rank, offs, ons, cores, topo)
            for name, view in (("xc%d" % j, T.xq[:, tok(j)].bitcast(dt.uint8)), ("xp%d" % j, T.xs[:, tok(j)])):
                if j != rank:
                    g.wait_ge(S[name], expect[(rank, j)])
                tr = []
                for m, ds in ((m_off, offs), (m_on, ons)):
                    if ds:
                        tr.append(RemoteDMATransfer(dst_ids=[did(d) for d in ds], dma_engine_mask=m,
                                                    remote_sem=S[name], srcs=[view], dsts=[view] * len(ds),
                                                    alu_op=0))
                        sent += _count(m)
                g.remote_dma_fused(tr, local_sem=S.sent)
        elif act[0] == "part":
            k = act[1]
            c0, c1 = span[k]
            g.wait_ge(S["loc%d" % k], 1)
            rid, pid, _ = topo.addr(cores[mate])
            m = topo.mask(core, cores[mate])
            g.remote_dma(T.lp[:, c0:c1], T.pe[:, c0:c1], S["sp%d" % k], S.sent, pid, rid, m)
            sent += _count(m)
        else:
            k = act[1]
            g.wait_ge(S["loc%d" % k], 1)
            offs = [r for r in range(N) if topo.chip(cores[r]) != ch]
            m_off, m_on = _masks(rank, offs, [mate], cores, topo)
            tr = []
            for m, ds in ((m_off, offs), (m_on, [mate])):
                tr.append(RemoteDMATransfer(dst_ids=[did(d) for d in ds], dma_engine_mask=m,
                                            remote_sem=S["sr%d_%d" % (k, ci)],
                                            srcs=[slot(k, ci)], dsts=[slot(k, ci)] * len(ds), alu_op=0))
                sent += _count(m)
            g.remote_dma_fused(tr, local_sem=S.sent)
    g.wait_ge(S.sent, sent)

    nv = [0]

    def vsem():
        nv[0] += 1
        return S["v%d" % (nv[0] - 1)]

    def sum_count(src_chip, dst_rank):
        s = P["far"][src_chip]
        offs = [r for r in range(N) if topo.chip(cores[r]) != src_chip]
        m_off, m_on = _masks(s, offs, [P["near"][src_chip]], cores, topo)
        return _count(m_on) if topo.chip(cores[dst_rank]) == src_chip else _count(m_off)

    e0, e1 = span[0]
    held = slot(0, ci) if is_far else T.pe[:, e0:e1]
    rho, rho2 = (T.tmp[:, N * i + e0:N * i + e1] for i in (4, 9))
    for k, grp in enumerate(groups):
        c0, c1 = span[k]
        for j in grp:
            ve.wait_ge(S["sq%d" % j], 1)
        if is_far:
            ve.wait_ge(S["sp%d" % k], _count(topo.mask(cores[mate], core)))
            ve.tensor_tensor(slot(k, ci), T.part[:, c0:c1], T.lp[:, c0:c1], ADD).then_inc(S["loc%d" % k], 1)
        else:
            ve.tensor_scalar(T.pe[:, c0:c1], T.part[:, c0:c1], EPS * DOWN / len(chips), None,
                             ADD).then_inc(S["loc%d" % k], 1)
        if k == 0:
            ve.wait_ge(S.er, 1)
            sa = vsem()
            ve.reciprocal(rho, T.er[:, e0:e1]).then_inc(sa, 1)
            ve.wait_ge(sa, 1)
            sb = vsem()
            ve.tensor_tensor(rho2, rho, rho, MUL).then_inc(sb, 1)
            ve.wait_ge(sb, 1)

    tot_sem, tot_need, f_sem, tot_ap = {}, {}, {}, {}
    R = math.sqrt(DOWN)
    H = W // 2
    for k, grp in enumerate(groups):
        c0, c1 = span[k]

        def tv(i):
            return T.tmp[:, N * i + c0:N * i + c1]

        for oi, o in enumerate(chips):
            if o == ch and is_far:
                ve.wait_ge(S["loc%d" % k], 1)
            else:
                ve.wait_ge(S["sr%d_%d" % (k, oi)], sum_count(o, rank))
        s = vsem()
        ve.tensor_tensor(T.tw[:, H * k:H * k + H], T.L[:, W * k:W * k + H], T.L[:, W * k + H:W * k + W],
                         ADD).then_inc(s, 1)
        ve.wait_ge(s, 1)
        s = vsem()
        acc = tv(11)
        if k == 0:
            for i in range(G):
                a = H * k + i
                ve.tensor_scalar(T.tmp[:, N * 11 + c0 + i:N * 11 + c0 + i + 1], T.tw[:, a:a + 1], T.tw[:, a + G:a + G + 1],
                                 T.tmp[:, N * 9 + e0 + i:N * 9 + e0 + i + 1], ADD, MUL).then_inc(s, 1)
            need = G
        else:
            ve.tensor_tensor(acc, T.tw[:, H * k:H * k + G], T.tw[:, H * k + G:H * k + H], ADD).then_inc(s, 1)
            need = 1
        tot_sem[k], tot_need[k], tot_ap[k] = s, need, acc
        ve.wait_ge(s, need)
        s1 = vsem()
        ve.reciprocal(tv(5), acc).then_inc(s1, 1)
        ve.wait_ge(s1, 1)
        ve.wait_ge(S["sd%d" % k], 1)
        s2 = vsem()
        ve.tensor_tensor(tv(6), T.sd[:, c0:c1], tv(5), MUL).then_inc(s2, 1)
        ve.wait_ge(s2, 1)
        s3 = vsem()
        ve.tensor_tensor(tv(7), tv(6), T.sd[:, c0:c1], MUL).then_inc(s3, 1)
        lead = tv(6)
        if k == 0:
            s6 = vsem()
            ve.tensor_tensor(tv(12), tv(6), rho, MUL).then_inc(s6, 1)
            lead = tv(12)
        ve.wait_ge(s3, 1)
        s4 = vsem()
        ve.tensor_scalar(tv(8), tv(7), -0.5 * R, 1.5 * R, MUL, ADD).then_inc(s4, 1)
        ve.wait_ge(s4, 1)
        if k == 0:
            ve.wait_ge(s6, 1)
        s5 = vsem()
        ve.tensor_tensor(tv(10), lead, tv(8), MUL).then_inc(s5, 1)
        f_sem[k] = s5
        ve.wait_ge(s5, 1)
        for i, j in enumerate(grp):
            if i % 2 == 0:
                c = N * 10 + col[j]
                ve.tensor_scalar(T.yb[:, blk(j)], T.z[:, blk(j)], T.tmp[:, c:c + 1], None,
                                 MUL).then_inc(S["sc%d" % j], 1)

    last0 = max(order.index(j) for j in groups[0])
    for n_, j in enumerate(order):
        sc.wait_ge(S["mm%d" % j], 1)
        sc.activation(T.junk[:, blk(j)], T.z[:, blk(j)], ActivationFunctionType.Square,
                      scale=math.sqrt(DOWN / (N * NC)), accum_out=T.part[:, col[j]:col[j] + 1]).then_inc(S["sq%d" % j], 1)
        if n_ == last0:
            sc.wait_ge(S.loc0, 1)
            sc.activation(T.er[:, e0:e1], held, ActivationFunctionType.Sqrt, bias=FLOOR).then_inc(S.er, 1)
    for k, grp in enumerate(groups):
        c0, c1 = span[k]
        sc.wait_ge(tot_sem[k], tot_need[k])
        sc.activation(T.sd[:, c0:c1], tot_ap[k], ActivationFunctionType.Sqrt).then_inc(S["sd%d" % k], 1)
        sc.wait_ge(f_sem[k], 1)
        for i, j in enumerate(grp):
            if i % 2 == 1:
                c = N * 10 + col[j]
                sc.activation(T.yb[:, blk(j)], T.z[:, blk(j)], ActivationFunctionType.Copy,
                              scale=T.tmp[:, c:c + 1]).then_inc(S["sc%d" % j], 1)

    st = 0
    for grp in groups:
        for i in range(0, len(grp), 2):
            pair = grp[i:i + 2]
            for j in pair:
                sy.wait_ge(S["sc%d" % j], 1)
            if len(pair) == 2 and pair[1] == pair[0] + 1:
                lo, hi = NC * pair[0], NC * pair[1] + NC
                sy.dma_start(T.y[:, lo:hi], T.yb[:, lo:hi]).then_inc(S.st, 16)
                st += 16
            else:
                for j in pair:
                    sy.dma_start(T.y[:, blk(j)], T.yb[:, blk(j)]).then_inc(S.st, 16)
                    st += 16
    sy.wait_ge(S.st, st)
